import numpy as np
import ml_dtypes


def mxq(x, axis, fmt="e4m3"):
    dtype, down = {"e4m3": (ml_dtypes.float8_e4m3fn, 7), "e5m2": (ml_dtypes.float8_e5m2, 14)}[fmt]
    v = np.moveaxis(np.asarray(x, np.float32).astype(ml_dtypes.bfloat16).astype(np.float64), axis, -1)
    blocks = v.reshape(v.shape[:-1] + (-1, 32))
    amax = np.abs(blocks).max(-1, keepdims=True)
    byte = np.maximum(np.where(amax > 0, np.frexp(amax)[1] - 1 + 127, 0) - down, 1)
    scale = np.exp2(byte - 127.0)
    codes = (blocks / scale).astype(np.float32).astype(dtype).astype(np.float64)
    return np.moveaxis((codes * scale).reshape(v.shape), -1, axis)


WIDE = False


def mx_kscale(k):
    if not WIDE:
        return np.ones(k)
    levels = np.array([10, -10, 5, -5, 0])
    if k % 512:
        return np.exp2(np.random.permutation(np.resize(levels, k // 32))).repeat(32)
    a = np.empty((k // 512, 16))
    for p in range(k // 512):
        a[p, :8] = np.random.permutation(np.resize(levels, 8))
        for g in range(8):
            far = levels[np.abs(levels - a[p, g]) >= 10]
            a[p, g + 8] = far[np.random.randint(len(far))]
    return np.exp2(a.ravel()).repeat(32)


def f64(x):
    return np.asarray(x).astype(np.float64)


def striped(idx):
    return np.tile(np.asarray(idx).reshape(-1, 16).T, (8, 1)).astype(np.uint16)


def unstriped(offs):
    return offs[:16].T.reshape(-1).astype(np.int64)


D, T, I, Q = 512, 1024, 512, 256


def setup_inputs():
    n = np.random.standard_normal
    idx = np.random.permutation(T)[:I]
    idx2 = np.random.permutation(T)[:I]
    fd = mx_kscale(D)
    return {
        "query": (n((D, Q)) * 0.8 / np.sqrt(D) * fd[:, None]).astype(np.float32),
        "keys": (n((D, T)) / fd[:, None]).astype(np.float32),
        "mass": np.tile(np.random.uniform(0.5, 4.0, T), (128, 1)).astype(np.float32),
        "offs": striped(idx),
        "offs2": striped(idx2),
    }


def reference(query, keys, mass, offs, offs2):
    idx = unstriped(offs)
    idx2 = unstriped(offs2)
    km = (f64(keys)[:, idx] * f64(mass)[:1][:, idx] + f64(keys)[:, idx2] * f64(mass)[:1][:, idx2]) / (f64(mass)[:1][:, idx] + f64(mass)[:1][:, idx2])
    queryq = mxq(f64(query), 0, "e4m3")
    kmq = mxq(km, 0, "e4m3")
    a = queryq.T @ kmq
    s = a + np.log(f64(mass)[:1][:, idx] + f64(mass)[:1][:, idx2])
    p = np.exp(s - np.max(s, axis=1, keepdims=True))
    y = p / np.sum(p, axis=1, keepdims=True) * 512.0
    return y

@@ -1,0 +1,161 @@
+from contextlib import ExitStack
+
+import concourse.mybir as mybir
+from concourse.masks import make_identity
+
+D, T, I, Q = 512, 1024, 512, 256
+FLOPS = 2 * D * I * Q
+
+F32 = mybir.dt.float32
+BF16 = mybir.dt.bfloat16
+U32 = mybir.dt.uint32
+U16 = mybir.dt.uint16
+U8 = mybir.dt.uint8
+FP8X4 = mybir.dt.float8_e4m3fn_x4
+ALU = mybir.AluOpType
+ACT = mybir.ActivationFunctionType
+
+P = 128
+PACK = 4
+BANK = 512
+CHUNKS = [(0, 256), (256, 128), (384, 128)]
+
+
+def tile_attend_massmerge_kernel(tc, query, keys, mass, offs, offs2, out):
+    nc = tc.nc
+    with ExitStack() as ctx:
+        sb = ctx.enter_context(tc.tile_pool(name="sb", bufs=1))
+        ps = ctx.enter_context(tc.psum_pool(name="ps", bufs=1))
+
+        def bank(number, name):
+            return ps.tile([P, BANK], F32, tag="bank%d" % number, name=name)
+
+        def sbuf(shape, dtype, name, tag=None):
+            return sb.tile(shape, dtype, name=name, tag=tag or name, align_bytes=64)
+
+        mass_sb = sbuf([P, T], F32, "mass_sb")
+        nc.sync.dma_start(mass_sb[:], mass)
+        lists = []
+        for name, src in (("list1", offs), ("list2", offs2)):
+            lst = sbuf([P, I // 16], U16, name)
+            nc.sync.dma_start(lst[:], src)
+            lists.append(lst)
+        key_rows = keys.rearrange("(p t) n -> t p n", t=PACK)
+        planes = []
+        for t in range(PACK):
+            plane = sbuf([P, T], F32, "plane%d" % t)
+            nc.sync.dma_start(plane[:], key_rows[t])
+            planes.append(plane)
+        q_raw = sbuf([P, PACK, Q], F32, "q_raw")
+        nc.sync.dma_start(q_raw[:], query.rearrange("(p t) n -> p t n", t=PACK))
+
+        ident = sbuf([P, P], F32, "ident")
+        make_identity(nc, ident[:])
+
+        picked = []
+        for l in range(2):
+            m = sbuf([P, I], F32, "picked%d" % l)
+            nc.vector.tensor_copy(m[:], mass_sb[:].indirect(lists[l][:]))
+            picked.append(m)
+        joint_t = bank(0, "joint_t")
+        for j in range(I // P):
+            cols = slice(j * P, (j + 1) * P)
+            for l in range(2):
+                nc.tensor.matmul(joint_t[:, cols], picked[l][:, cols], ident[:],
+                                 start=(l == 0), stop=(l == 1), is_transpose=True)
+        joint_col = joint_t[:].rearrange("s (j x) -> s j x", x=P)[:, :, 0]
+        log_col = sbuf([P, I // P], F32, "log_col")
+        nc.scalar.activation(log_col[:], joint_col, ACT.Ln)
+        inv = sbuf([P, I // P], F32, "inv")
+        nc.vector.reciprocal(inv[:], joint_col)
+        warm = sbuf([P, 1], F32, "warm")
+        nc.scalar.activation(warm[:], log_col[:, 0:1], ACT.Exp)
+        log_ps = bank(1, "log_ps")
+        for j in range(I // P):
+            nc.tensor.transpose(log_ps[:, j * P:(j + 1) * P], log_col[:, j:j + 1].to_broadcast([P, P]), ident[:])
+        log_row = sbuf([P, I], F32, "log_row")
+        nc.scalar.copy(log_row[:], log_ps[:])
+
+        neg = [sbuf([P, I], F32, "neg%d" % h) for h in range(2)]
+        low = [None, None]
+        score_bank = [0, 1, 3]
+        last = len(CHUNKS) - 1
+        late = None
+        q_bf = None
+        q_codes = None
+        q_scales = None
+        for c, (first, n) in enumerate(CHUNKS):
+            slots = slice(first, first + n)
+            entries = slice(first // 16, (first + n) // 16)
+            blocks = range(first // P, (first + n) // P)
+            if c == 1:
+                late = sbuf([P, 2 * 2 * PACK, P], F32, "late", "hold")
+            back = {j: bank(6 + j % 2, "back%d" % j) for j in blocks}
+            stages = [(0,), (1,)] if c == last else [(0, 1)]
+            for halves in stages:
+                sums = {j: bank(2 if halves == (1,) else 2 + j, "sums%d_%d" % (j, halves[0])) for j in blocks}
+                for t in range(2 * halves[0], 2 * halves[-1] + 2):
+                    for l in range(2):
+                        if c == 0:
+                            g_tile = sbuf([P, n], F32, "g%d_%d" % (t, l), "hold" if (t, l) == (3, 0) else None)
+                            g = g_tile[:]
+                        else:
+                            g = late[:, (c - 1) * 2 * PACK + 2 * t + l, :]
+                        nc.vector.tensor_tensor(g, planes[t][:].indirect(lists[l][:, entries]),
+                                                picked[l][:, slots], ALU.mult)
+                        for j in blocks:
+                            nc.tensor.matmul(sums[j][:, t * P:(t + 1) * P],
+                                             g[:, j * P - first:(j + 1) * P - first], ident[:],
+                                             start=(l == 0), stop=(l == 1), is_transpose=True)
+                if c == 0:
+                    q_bf = sbuf([P, Q, PACK], BF16, "q_bf", "g1_1")
+                    nc.scalar.copy(q_bf[:], q_raw[:].rearrange("p t n -> p n t"))
+                for j in blocks:
+                    k = len(halves)
+                    pairs = sbuf([P, k, P, 2], BF16, "pairs%d_%d" % (j, halves[0]))
+                    nc.scalar.activation(
+                        pairs[:],
+                        sums[j][:, 2 * halves[0] * P:2 * (halves[-1] + 1) * P].rearrange("s (u e p) -> s u p e", u=k, e=2),
+                        ACT.Copy, scale=inv[:, j:j + 1])
+                    words = pairs[:].rearrange("s u p e -> s (u p e)").bitcast(F32)
+                    for i, u in enumerate(halves):
+                        nc.tensor.transpose(back[j][:, u * P:(u + 1) * P], words[:, i * P:(i + 1) * P], ident[:])
+            km = sbuf([P, n * PACK], BF16, "km%d" % c)
+            km_words = km[:].bitcast(F32).rearrange("p (s u) -> p s u", u=2)
+            for j in blocks:
+                nc.scalar.copy(km_words[:, j * P - first:(j + 1) * P - first, :],
+                               back[j][:, 0:2 * P].rearrange("p (u s) -> p s u", u=2))
+            if c == 0:
+                q_codes = sbuf([P, Q], U32, "q_codes", "pairs0_0")
+                q_scales = sbuf([P, Q], U8, "q_scales")
+                nc.vector.quantize_mx(out=q_codes[:].bitcast(FP8X4), scales=q_scales[:],
+                                      in_=q_bf[:].rearrange("p n t -> p (n t)"))
+            k_codes = sbuf([P, n], U32, "k_codes%d" % c)
+            k_scales = sbuf([P, n], U8, "k_scales%d" % c)
+            nc.vector.quantize_mx(out=k_codes[:].bitcast(FP8X4), scales=k_scales[:], in_=km[:])
+            scores = bank(score_bank[c], "scores%d" % c)
+            for h in range(2):
+                rows = slice(h * P, (h + 1) * P)
+                nc.tensor.matmul_mx(out=scores[:, h * n:(h + 1) * n],
+                                    lhsT=q_codes[:, rows].bitcast(FP8X4), lhsT_scale=q_scales[:, rows],
+                                    rhs=k_codes[:].bitcast(FP8X4), rhs_scale=k_scales[:],
+                                    start=True, stop=True)
+            biased = sbuf([P, 2, n], F32, "biased%d" % c)
+            for h in range(2):
+                nc.vector.tensor_tensor(biased[:, h, :], scores[:, h * n:(h + 1) * n], log_row[:, slots], ALU.add)
+            for h in range(2):
+                new_low = sbuf([P, 1], F32, "low%d_%d" % (c, h))
+                start_value = None if c == 0 else low[h][:]
+                nc.vector.tensor_scalar(neg[h][:, slots], biased[:, h, :], -1.0, start_value,
+                                        ALU.mult, ALU.min, accum_out=new_low[:])
+                low[h] = new_low
+
+        for h in range(2):
+            expd = sbuf([P, I], F32, "expd%d" % h)
+            total = sbuf([P, 1], F32, "total%d" % h)
+            nc.scalar.activation(expd[:], neg[h][:], ACT.Exp, bias=low[h][:], scale=-1.0, accum_out=total[:])
+            share = sbuf([P, 1], F32, "share%d" % h)
+            nc.vector.reciprocal(share[:], total[:])
+            res = sbuf([P, I], F32, "res%d" % h)
+            nc.vector.tensor_scalar(res[:], expd[:], share[:], 512.0, ALU.mult, ALU.mult)
+            nc.sync.dma_start(out[h * P:(h + 1) * P, :], res[:])

@@ -58,11 +58,11 @@ def tile_attend_massmerge_kernel(tc, query, keys, mass, offs, offs2, out):
             nc.vector.tensor_copy(m[:], mass_sb[:].indirect(lists[l][:]))
             picked.append(m)
         joint_t = bank(0, "joint_t")
-        for j in range(I // P):
-            cols = slice(j * P, (j + 1) * P)
-            for l in range(2):
+        for l in range(2):
+            for j in range(I // P):
+                cols = slice(j * P, (j + 1) * P)
                 nc.tensor.matmul(joint_t[:, cols], picked[l][:, cols], ident[:],
-                                 start=(l == 0), stop=(l == 1), is_transpose=True)
+                                 start=(l, j) == (0, 0), stop=(l, j) == (1, I // P - 1), is_transpose=True)
         joint_col = joint_t[:].rearrange("s (j x) -> s j x", x=P)[:, :, 0]
         log_col = sbuf([P, I // P], F32, "log_col")
         nc.scalar.activation(log_col[:], joint_col, ACT.Ln)
@@ -79,47 +79,64 @@ def tile_attend_massmerge_kernel(tc, query, keys, mass, offs, offs2, out):
         neg = [sbuf([P, I], F32, "neg%d" % h) for h in range(2)]
         low = [None, None]
         score_bank = [0, 1, 3]
-        last = len(CHUNKS) - 1
         late = None
+        used = 0
         q_bf = None
         q_codes = None
         q_scales = None
+        sums = {}
+        back = {}
+
+        def round_and_turn_back(j, halves):
+            k = len(halves)
+            pairs = sbuf([P, k, P, 2], BF16, "pairs%d_%d" % (j, halves[0]))
+            nc.scalar.activation(
+                pairs[:],
+                sums[(j, halves[0])][:, 2 * halves[0] * P:2 * (halves[-1] + 1) * P].rearrange("s (u e p) -> s u p e", u=k, e=2),
+                ACT.Copy, scale=inv[:, j:j + 1])
+            words = pairs[:].rearrange("s u p e -> s (u p e)").bitcast(F32)
+            if halves[0] == 0:
+                back[j] = bank(6 + j % 2, "back%d" % j)
+            for i, u in enumerate(halves):
+                nc.tensor.transpose(back[j][:, u * P:(u + 1) * P], words[:, i * P:(i + 1) * P], ident[:])
+
         for c, (first, n) in enumerate(CHUNKS):
             slots = slice(first, first + n)
-            entries = slice(first // 16, (first + n) // 16)
             blocks = range(first // P, (first + n) // P)
             if c == 1:
-                late = sbuf([P, 2 * 2 * PACK, P], F32, "late", "hold")
-            back = {j: bank(6 + j % 2, "back%d" % j) for j in blocks}
-            stages = [(0,), (1,)] if c == last else [(0, 1)]
-            for halves in stages:
-                sums = {j: bank(2 if halves == (1,) else 2 + j, "sums%d_%d" % (j, halves[0])) for j in blocks}
-                for t in range(2 * halves[0], 2 * halves[-1] + 2):
+                late = sbuf([P, 2 * 2 * PACK * P], F32, "late", "hold")
+            runs = [[(0, 256, (0, 1, 2, 3))], [(256, 256, (0, 1)), (256, 128, (2, 3))], [(384, 128, (2, 3))]][c]
+            for start, width, ts in runs:
+                run_blocks = range(start // P, (start + width) // P)
+                for j in run_blocks:
+                    if ts[0] == 0:
+                        sums[(j, 0)] = bank(2 + j, "sums%d_0" % j)
+                    elif j == 3:
+                        sums[(j, 1)] = bank(2, "sums3_1")
+                    if j != 3:
+                        sums[(j, 1)] = sums[(j, 0)]
+                for t in ts:
                     for l in range(2):
                         if c == 0:
-                            g_tile = sbuf([P, n], F32, "g%d_%d" % (t, l), "hold" if (t, l) == (3, 0) else None)
+                            g_tile = sbuf([P, width], F32, "g%d_%d" % (t, l), "hold" if (t, l) == (3, 0) else None)
                             g = g_tile[:]
                         else:
-                            g = late[:, (c - 1) * 2 * PACK + 2 * t + l, :]
-                        nc.vector.tensor_tensor(g, planes[t][:].indirect(lists[l][:, entries]),
-                                                picked[l][:, slots], ALU.mult)
-                        for j in blocks:
-                            nc.tensor.matmul(sums[j][:, t * P:(t + 1) * P],
-                                             g[:, j * P - first:(j + 1) * P - first], ident[:],
+                            g = late[:, used:used + width]
+                            used = used + width
+                        nc.vector.tensor_tensor(g, planes[t][:].indirect(lists[l][:, start // 16:(start + width) // 16]),
+                                                picked[l][:, start:start + width], ALU.mult)
+                        for j in run_blocks:
+                            nc.tensor.matmul(sums[(j, t // 2)][:, t * P:(t + 1) * P],
+                                             g[:, j * P - start:(j + 1) * P - start], ident[:],
                                              start=(l == 0), stop=(l == 1), is_transpose=True)
                 if c == 0:
                     q_bf = sbuf([P, Q, PACK], BF16, "q_bf", "g1_1")
                     nc.scalar.copy(q_bf[:], q_raw[:].rearrange("p t n -> p n t"))
-                for j in blocks:
-                    k = len(halves)
-                    pairs = sbuf([P, k, P, 2], BF16, "pairs%d_%d" % (j, halves[0]))
-                    nc.scalar.activation(
-                        pairs[:],
-                        sums[j][:, 2 * halves[0] * P:2 * (halves[-1] + 1) * P].rearrange("s (u e p) -> s u p e", u=k, e=2),
-                        ACT.Copy, scale=inv[:, j:j + 1])
-                    words = pairs[:].rearrange("s u p e -> s (u p e)").bitcast(F32)
-                    for i, u in enumerate(halves):
-                        nc.tensor.transpose(back[j][:, u * P:(u + 1) * P], words[:, i * P:(i + 1) * P], ident[:])
+                for j in run_blocks:
+                    if j == 3:
+                        round_and_turn_back(j, (ts[0] // 2,))
+                    elif ts[-1] == 3:
+                        round_and_turn_back(j, (0, 1))
             km = sbuf([P, n * PACK], BF16, "km%d" % c)
             km_words = km[:].bitcast(F32).rearrange("p (s u) -> p s u", u=2)
             for j in blocks:
@@ -157,5 +174,7 @@ def tile_attend_massmerge_kernel(tc, query, keys, mass, offs, offs2, out):
             share = sbuf([P, 1], F32, "share%d" % h)
             nc.vector.reciprocal(share[:], total[:])
             res = sbuf([P, I], F32, "res%d" % h)
-            nc.vector.tensor_scalar(res[:], expd[:], share[:], 512.0, ALU.mult, ALU.mult)
-            nc.sync.dma_start(out[h * P:(h + 1) * P, :], res[:])
+            pieces = [(0, I, nc.sync)] if h == 0 else [(0, I // 2, nc.scalar), (I // 2, I, nc.sync)]
+            for lo, hi, queue in pieces:
+                nc.vector.tensor_scalar(res[:, lo:hi], expd[:, lo:hi], share[:], 512.0, ALU.mult, ALU.mult)
+                queue.dma_start(out[h * P:(h + 1) * P, lo:hi], res[:, lo:hi])

@@ -174,7 +174,5 @@ def tile_attend_massmerge_kernel(tc, query, keys, mass, offs, offs2, out):
             share = sbuf([P, 1], F32, "share%d" % h)
             nc.vector.reciprocal(share[:], total[:])
             res = sbuf([P, I], F32, "res%d" % h)
-            pieces = [(0, I, nc.sync)] if h == 0 else [(0, I // 2, nc.scalar), (I // 2, I, nc.sync)]
-            for lo, hi, queue in pieces:
-                nc.vector.tensor_scalar(res[:, lo:hi], expd[:, lo:hi], share[:], 512.0, ALU.mult, ALU.mult)
-                queue.dma_start(out[h * P:(h + 1) * P, lo:hi], res[:, lo:hi])
+            nc.vector.tensor_scalar(res[:], expd[:], share[:], 512.0, ALU.mult, ALU.mult)
+            nc.sync.dma_start(out[h * P:(h + 1) * P, :], res[:])

@@ -17,8 +17,20 @@ ACT = mybir.ActivationFunctionType
 
 P = 128
 PACK = 4
+LISTS = 2
+ENTRIES_PER_COLUMN = 16
 BANK = 512
+BLOCKS = I // P
+ROW_TILES = Q // P
+OUT_SCALE = 512.0
+
 CHUNKS = [(0, 256), (256, 128), (384, 128)]
+
+JOINT_BANK = 0
+LOG_BANK = 1
+SUM_BANK = 2
+BACK_BANK = 6
+SCORE_BANKS = [JOINT_BANK, LOG_BANK, SUM_BANK + 1]
 
 
 def tile_attend_massmerge_kernel(tc, query, keys, mass, offs, offs2, out):
@@ -37,7 +49,7 @@ def tile_attend_massmerge_kernel(tc, query, keys, mass, offs, offs2, out):
         nc.sync.dma_start(mass_sb[:], mass)
         lists = []
         for name, src in (("list1", offs), ("list2", offs2)):
-            lst = sbuf([P, I // 16], U16, name)
+            lst = sbuf([P, I // ENTRIES_PER_COLUMN], U16, name)
             nc.sync.dma_start(lst[:], src)
             lists.append(lst)
         key_rows = keys.rearrange("(p t) n -> t p n", t=PACK)
@@ -53,90 +65,74 @@ def tile_attend_massmerge_kernel(tc, query, keys, mass, offs, offs2, out):
         make_identity(nc, ident[:])
 
         picked = []
-        for l in range(2):
+        for l in range(LISTS):
             m = sbuf([P, I], F32, "picked%d" % l)
             nc.vector.tensor_copy(m[:], mass_sb[:].indirect(lists[l][:]))
             picked.append(m)
-        joint_t = bank(0, "joint_t")
-        for l in range(2):
-            for j in range(I // P):
+
+        joint_t = bank(JOINT_BANK, "joint_t")
+        for l in range(LISTS):
+            for j in range(BLOCKS):
                 cols = slice(j * P, (j + 1) * P)
                 nc.tensor.matmul(joint_t[:, cols], picked[l][:, cols], ident[:],
-                                 start=(l, j) == (0, 0), stop=(l, j) == (1, I // P - 1), is_transpose=True)
+                                 start=(l, j) == (0, 0), stop=(l, j) == (LISTS - 1, BLOCKS - 1),
+                                 is_transpose=True)
         joint_col = joint_t[:].rearrange("s (j x) -> s j x", x=P)[:, :, 0]
-        log_col = sbuf([P, I // P], F32, "log_col")
+        log_col = sbuf([P, BLOCKS], F32, "log_col")
         nc.scalar.activation(log_col[:], joint_col, ACT.Ln)
-        inv = sbuf([P, I // P], F32, "inv")
+        inv = sbuf([P, BLOCKS], F32, "inv")
         nc.vector.reciprocal(inv[:], joint_col)
-        warm = sbuf([P, 1], F32, "warm")
-        nc.scalar.activation(warm[:], log_col[:, 0:1], ACT.Exp)
-        log_ps = bank(1, "log_ps")
-        for j in range(I // P):
+
+        log_ps = bank(LOG_BANK, "log_ps")
+        for j in range(BLOCKS):
             nc.tensor.transpose(log_ps[:, j * P:(j + 1) * P], log_col[:, j:j + 1].to_broadcast([P, P]), ident[:])
         log_row = sbuf([P, I], F32, "log_row")
         nc.scalar.copy(log_row[:], log_ps[:])
 
-        neg = [sbuf([P, I], F32, "neg%d" % h) for h in range(2)]
-        low = [None, None]
-        score_bank = [0, 1, 3]
-        late = None
-        used = 0
-        q_bf = None
-        q_codes = None
-        q_scales = None
-        sums = {}
-        back = {}
-
-        def round_and_turn_back(j, halves):
-            k = len(halves)
-            pairs = sbuf([P, k, P, 2], BF16, "pairs%d_%d" % (j, halves[0]))
-            nc.scalar.activation(
-                pairs[:],
-                sums[(j, halves[0])][:, 2 * halves[0] * P:2 * (halves[-1] + 1) * P].rearrange("s (u e p) -> s u p e", u=k, e=2),
-                ACT.Copy, scale=inv[:, j:j + 1])
-            words = pairs[:].rearrange("s u p e -> s (u p e)").bitcast(F32)
-            if halves[0] == 0:
-                back[j] = bank(6 + j % 2, "back%d" % j)
-            for i, u in enumerate(halves):
-                nc.tensor.transpose(back[j][:, u * P:(u + 1) * P], words[:, i * P:(i + 1) * P], ident[:])
-
+        neg = [sbuf([P, I], F32, "neg%d" % h) for h in range(ROW_TILES)]
+        low = [None] * ROW_TILES
+        last = len(CHUNKS) - 1
+        gathers_per_chunk = LISTS * PACK
         for c, (first, n) in enumerate(CHUNKS):
             slots = slice(first, first + n)
+            entries = slice(first // ENTRIES_PER_COLUMN, (first + n) // ENTRIES_PER_COLUMN)
             blocks = range(first // P, (first + n) // P)
             if c == 1:
-                late = sbuf([P, 2 * 2 * PACK * P], F32, "late", "hold")
-            runs = [[(0, 256, (0, 1, 2, 3))], [(256, 256, (0, 1)), (256, 128, (2, 3))], [(384, 128, (2, 3))]][c]
-            for start, width, ts in runs:
-                run_blocks = range(start // P, (start + width) // P)
-                for j in run_blocks:
-                    if ts[0] == 0:
-                        sums[(j, 0)] = bank(2 + j, "sums%d_0" % j)
-                    elif j == 3:
-                        sums[(j, 1)] = bank(2, "sums3_1")
-                    if j != 3:
-                        sums[(j, 1)] = sums[(j, 0)]
-                for t in ts:
-                    for l in range(2):
+                late = sbuf([P, last * gathers_per_chunk, P], F32, "late", "g2_1")
+            back = {j: bank(BACK_BANK + j % 2, "back%d" % j) for j in blocks}
+
+            stages = [(0,), (1,)] if c == last else [(0, 1)]
+            for halves in stages:
+                sums = {j: bank(SUM_BANK if halves == (1,) else SUM_BANK + j, "sums%d_%d" % (j, halves[0]))
+                        for j in blocks}
+                for t in range(2 * halves[0], 2 * halves[-1] + 2):
+                    for l in range(LISTS):
                         if c == 0:
-                            g_tile = sbuf([P, width], F32, "g%d_%d" % (t, l), "hold" if (t, l) == (3, 0) else None)
-                            g = g_tile[:]
+                            g = sbuf([P, n], F32, "g%d_%d" % (t, l))[:]
                         else:
-                            g = late[:, used:used + width]
-                            used = used + width
-                        nc.vector.tensor_tensor(g, planes[t][:].indirect(lists[l][:, start // 16:(start + width) // 16]),
-                                                picked[l][:, start:start + width], ALU.mult)
-                        for j in run_blocks:
-                            nc.tensor.matmul(sums[(j, t // 2)][:, t * P:(t + 1) * P],
-                                             g[:, j * P - start:(j + 1) * P - start], ident[:],
-                                             start=(l == 0), stop=(l == 1), is_transpose=True)
+                            g = late[:, (c - 1) * gathers_per_chunk + LISTS * t + l, :]
+                        nc.vector.tensor_tensor(g, planes[t][:].indirect(lists[l][:, entries]),
+                                                picked[l][:, slots], ALU.mult)
+                        for j in blocks:
+                            nc.tensor.matmul(sums[j][:, t * P:(t + 1) * P],
+                                             g[:, j * P - first:(j + 1) * P - first], ident[:],
+                                             start=(l == 0), stop=(l == LISTS - 1), is_transpose=True)
                 if c == 0:
                     q_bf = sbuf([P, Q, PACK], BF16, "q_bf", "g1_1")
                     nc.scalar.copy(q_bf[:], q_raw[:].rearrange("p t n -> p n t"))
-                for j in run_blocks:
-                    if j == 3:
-                        round_and_turn_back(j, (ts[0] // 2,))
-                    elif ts[-1] == 3:
-                        round_and_turn_back(j, (0, 1))
+                for j in blocks:
+                    k = len(halves)
+                    pairs = sbuf([P, k, P, 2], BF16, "pairs%d_%d" % (j, halves[0]))
+                    nc.scalar.activation(
+                        pairs[:],
+                        sums[j][:, 2 * halves[0] * P:2 * (halves[-1] + 1) * P].rearrange(
+                            "s (u e p) -> s u p e", u=k, e=2),
+                        ACT.Copy, scale=inv[:, j:j + 1])
+                    words = pairs[:].rearrange("s u p e -> s (u p e)").bitcast(F32)
+                    for place, u in enumerate(halves):
+                        nc.tensor.transpose(back[j][:, u * P:(u + 1) * P],
+                                            words[:, place * P:(place + 1) * P], ident[:])
+
             km = sbuf([P, n * PACK], BF16, "km%d" % c)
             km_words = km[:].bitcast(F32).rearrange("p (s u) -> p s u", u=2)
             for j in blocks:
@@ -150,29 +146,30 @@ def tile_attend_massmerge_kernel(tc, query, keys, mass, offs, offs2, out):
             k_codes = sbuf([P, n], U32, "k_codes%d" % c)
             k_scales = sbuf([P, n], U8, "k_scales%d" % c)
             nc.vector.quantize_mx(out=k_codes[:].bitcast(FP8X4), scales=k_scales[:], in_=km[:])
-            scores = bank(score_bank[c], "scores%d" % c)
-            for h in range(2):
+
+            scores = bank(SCORE_BANKS[c], "scores%d" % c)
+            for h in range(ROW_TILES):
                 rows = slice(h * P, (h + 1) * P)
                 nc.tensor.matmul_mx(out=scores[:, h * n:(h + 1) * n],
                                     lhsT=q_codes[:, rows].bitcast(FP8X4), lhsT_scale=q_scales[:, rows],
                                     rhs=k_codes[:].bitcast(FP8X4), rhs_scale=k_scales[:],
                                     start=True, stop=True)
-            biased = sbuf([P, 2, n], F32, "biased%d" % c)
-            for h in range(2):
+            biased = sbuf([P, ROW_TILES, n], F32, "biased%d" % c)
+            for h in range(ROW_TILES):
                 nc.vector.tensor_tensor(biased[:, h, :], scores[:, h * n:(h + 1) * n], log_row[:, slots], ALU.add)
-            for h in range(2):
+            for h in range(ROW_TILES):
                 new_low = sbuf([P, 1], F32, "low%d_%d" % (c, h))
                 start_value = None if c == 0 else low[h][:]
                 nc.vector.tensor_scalar(neg[h][:, slots], biased[:, h, :], -1.0, start_value,
                                         ALU.mult, ALU.min, accum_out=new_low[:])
                 low[h] = new_low
 
-        for h in range(2):
+        for h in range(ROW_TILES):
             expd = sbuf([P, I], F32, "expd%d" % h)
             total = sbuf([P, 1], F32, "total%d" % h)
             nc.scalar.activation(expd[:], neg[h][:], ACT.Exp, bias=low[h][:], scale=-1.0, accum_out=total[:])
             share = sbuf([P, 1], F32, "share%d" % h)
             nc.vector.reciprocal(share[:], total[:])
             res = sbuf([P, I], F32, "res%d" % h)
-            nc.vector.tensor_scalar(res[:], expd[:], share[:], 512.0, ALU.mult, ALU.mult)
+            nc.vector.tensor_scalar(res[:], expd[:], share[:], OUT_SCALE, ALU.mult, ALU.mult)
             nc.sync.dma_start(out[h * P:(h + 1) * P, :], res[:])

@@ -98,7 +98,7 @@ def tile_attend_massmerge_kernel(tc, query, keys, mass, offs, offs2, out):
             entries = slice(first // ENTRIES_PER_COLUMN, (first + n) // ENTRIES_PER_COLUMN)
             blocks = range(first // P, (first + n) // P)
             if c == 1:
-                late = sbuf([P, last * gathers_per_chunk, P], F32, "late", "g2_1")
+                late = sbuf([P, last * gathers_per_chunk, P], F32, "late", "g2_0")
             back = {j: bank(BACK_BANK + j % 2, "back%d" % j) for j in blocks}
 
             stages = [(0,), (1,)] if c == last else [(0, 1)]

from contextlib import ExitStack

import concourse.mybir as mybir
from concourse.masks import make_identity

D, T, I, Q = 512, 1024, 512, 256
FLOPS = 2 * D * I * Q

F32 = mybir.dt.float32
BF16 = mybir.dt.bfloat16
U32 = mybir.dt.uint32
U16 = mybir.dt.uint16
U8 = mybir.dt.uint8
FP8X4 = mybir.dt.float8_e4m3fn_x4
ALU = mybir.AluOpType
ACT = mybir.ActivationFunctionType

P = 128
PACK = 4
LISTS = 2
ENTRIES_PER_COLUMN = 16
BANK = 512
BLOCKS = I // P
ROW_TILES = Q // P
OUT_SCALE = 512.0

CHUNKS = [(0, 256), (256, 128), (384, 128)]

JOINT_BANK = 0
LOG_BANK = 1
SUM_BANK = 2
BACK_BANK = 6
SCORE_BANKS = [JOINT_BANK, LOG_BANK, SUM_BANK + 1]


def tile_attend_massmerge_kernel(tc, query, keys, mass, offs, offs2, out):
    nc = tc.nc
    with ExitStack() as ctx:
        sb = ctx.enter_context(tc.tile_pool(name="sb", bufs=1))
        ps = ctx.enter_context(tc.psum_pool(name="ps", bufs=1))

        def bank(number, name):
            return ps.tile([P, BANK], F32, tag="bank%d" % number, name=name)

        def sbuf(shape, dtype, name, tag=None):
            return sb.tile(shape, dtype, name=name, tag=tag or name, align_bytes=64)

        mass_sb = sbuf([P, T], F32, "mass_sb")
        nc.sync.dma_start(mass_sb[:], mass)
        lists = []
        for name, src in (("list1", offs), ("list2", offs2)):
            lst = sbuf([P, I // ENTRIES_PER_COLUMN], U16, name)
            nc.sync.dma_start(lst[:], src)
            lists.append(lst)
        key_rows = keys.rearrange("(p t) n -> t p n", t=PACK)
        planes = []
        for t in range(PACK):
            plane = sbuf([P, T], F32, "plane%d" % t)
            nc.sync.dma_start(plane[:], key_rows[t])
            planes.append(plane)
        q_raw = sbuf([P, PACK, Q], F32, "q_raw")
        nc.sync.dma_start(q_raw[:], query.rearrange("(p t) n -> p t n", t=PACK))

        ident = sbuf([P, P], F32, "ident")
        make_identity(nc, ident[:])

        picked = []
        for l in range(LISTS):
            m = sbuf([P, I], F32, "picked%d" % l)
            nc.vector.tensor_copy(m[:], mass_sb[:].indirect(lists[l][:]))
            picked.append(m)

        joint_t = bank(JOINT_BANK, "joint_t")
        for l in range(LISTS):
            for j in range(BLOCKS):
                cols = slice(j * P, (j + 1) * P)
                nc.tensor.matmul(joint_t[:, cols], picked[l][:, cols], ident[:],
                                 start=(l, j) == (0, 0), stop=(l, j) == (LISTS - 1, BLOCKS - 1),
                                 is_transpose=True)
        joint_col = joint_t[:].rearrange("s (j x) -> s j x", x=P)[:, :, 0]
        log_col = sbuf([P, BLOCKS], F32, "log_col")
        nc.scalar.activation(log_col[:], joint_col, ACT.Ln)
        inv = sbuf([P, BLOCKS], F32, "inv")
        nc.vector.reciprocal(inv[:], joint_col)

        log_ps = bank(LOG_BANK, "log_ps")
        for j in range(BLOCKS):
            nc.tensor.transpose(log_ps[:, j * P:(j + 1) * P], log_col[:, j:j + 1].to_broadcast([P, P]), ident[:])
        log_row = sbuf([P, I], F32, "log_row")
        nc.scalar.copy(log_row[:], log_ps[:])

        neg = [sbuf([P, I], F32, "neg%d" % h) for h in range(ROW_TILES)]
        low = [None] * ROW_TILES
        last = len(CHUNKS) - 1
        gathers_per_chunk = LISTS * PACK
        for c, (first, n) in enumerate(CHUNKS):
            slots = slice(first, first + n)
            entries = slice(first // ENTRIES_PER_COLUMN, (first + n) // ENTRIES_PER_COLUMN)
            blocks = range(first // P, (first + n) // P)
            if c == 1:
                late = sbuf([P, last * gathers_per_chunk, P], F32, "late", "g2_0")
            back = {j: bank(BACK_BANK + j % 2, "back%d" % j) for j in blocks}

            stages = [(0,), (1,)] if c == last else [(0, 1)]
            for halves in stages:
                sums = {j: bank(SUM_BANK if halves == (1,) else SUM_BANK + j, "sums%d_%d" % (j, halves[0]))
                        for j in blocks}
                for t in range(2 * halves[0], 2 * halves[-1] + 2):
                    for l in range(LISTS):
                        if c == 0:
                            g = sbuf([P, n], F32, "g%d_%d" % (t, l))[:]
                        else:
                            g = late[:, (c - 1) * gathers_per_chunk + LISTS * t + l, :]
                        nc.vector.tensor_tensor(g, planes[t][:].indirect(lists[l][:, entries]),
                                                picked[l][:, slots], ALU.mult)
                        for j in blocks:
                            nc.tensor.matmul(sums[j][:, t * P:(t + 1) * P],
                                             g[:, j * P - first:(j + 1) * P - first], ident[:],
                                             start=(l == 0), stop=(l == LISTS - 1), is_transpose=True)
                if c == 0:
                    q_bf = sbuf([P, Q, PACK], BF16, "q_bf", "g1_1")
                    nc.scalar.copy(q_bf[:], q_raw[:].rearrange("p t n -> p n t"))
                for j in blocks:
                    k = len(halves)
                    pairs = sbuf([P, k, P, 2], BF16, "pairs%d_%d" % (j, halves[0]))
                    nc.scalar.activation(
                        pairs[:],
                        sums[j][:, 2 * halves[0] * P:2 * (halves[-1] + 1) * P].rearrange(
                            "s (u e p) -> s u p e", u=k, e=2),
                        ACT.Copy, scale=inv[:, j:j + 1])
                    words = pairs[:].rearrange("s u p e -> s (u p e)").bitcast(F32)
                    for place, u in enumerate(halves):
                        nc.tensor.transpose(back[j][:, u * P:(u + 1) * P],
                                            words[:, place * P:(place + 1) * P], ident[:])

            km = sbuf([P, n * PACK], BF16, "km%d" % c)
            km_words = km[:].bitcast(F32).rearrange("p (s u) -> p s u", u=2)
            for j in blocks:
                nc.scalar.copy(km_words[:, j * P - first:(j + 1) * P - first, :],
                               back[j][:, 0:2 * P].rearrange("p (u s) -> p s u", u=2))
            if c == 0:
                q_codes = sbuf([P, Q], U32, "q_codes", "pairs0_0")
                q_scales = sbuf([P, Q], U8, "q_scales")
                nc.vector.quantize_mx(out=q_codes[:].bitcast(FP8X4), scales=q_scales[:],
                                      in_=q_bf[:].rearrange("p n t -> p (n t)"))
            k_codes = sbuf([P, n], U32, "k_codes%d" % c)
            k_scales = sbuf([P, n], U8, "k_scales%d" % c)
            nc.vector.quantize_mx(out=k_codes[:].bitcast(FP8X4), scales=k_scales[:], in_=km[:])

            scores = bank(SCORE_BANKS[c], "scores%d" % c)
            for h in range(ROW_TILES):
                rows = slice(h * P, (h + 1) * P)
                nc.tensor.matmul_mx(out=scores[:, h * n:(h + 1) * n],
                                    lhsT=q_codes[:, rows].bitcast(FP8X4), lhsT_scale=q_scales[:, rows],
                                    rhs=k_codes[:].bitcast(FP8X4), rhs_scale=k_scales[:],
                                    start=True, stop=True)
            biased = sbuf([P, ROW_TILES, n], F32, "biased%d" % c)
            for h in range(ROW_TILES):
                nc.vector.tensor_tensor(biased[:, h, :], scores[:, h * n:(h + 1) * n], log_row[:, slots], ALU.add)
            for h in range(ROW_TILES):
                new_low = sbuf([P, 1], F32, "low%d_%d" % (c, h))
                start_value = None if c == 0 else low[h][:]
                nc.vector.tensor_scalar(neg[h][:, slots], biased[:, h, :], -1.0, start_value,
                                        ALU.mult, ALU.min, accum_out=new_low[:])
                low[h] = new_low

        for h in range(ROW_TILES):
            expd = sbuf([P, I], F32, "expd%d" % h)
            total = sbuf([P, 1], F32, "total%d" % h)
            nc.scalar.activation(expd[:], neg[h][:], ACT.Exp, bias=low[h][:], scale=-1.0, accum_out=total[:])
            share = sbuf([P, 1], F32, "share%d" % h)
            nc.vector.reciprocal(share[:], total[:])
            res = sbuf([P, I], F32, "res%d" % h)
            nc.vector.tensor_scalar(res[:], expd[:], share[:], OUT_SCALE, ALU.mult, ALU.mult)
            nc.sync.dma_start(out[h * P:(h + 1) * P, :], res[:])
